import numpy as np, ml_dtypes
CORES = [40,41,42,43,44,45,46,47]
N = 8
import mx_ref
BF = ml_dtypes.bfloat16
def cols(t, e):
    v = np.concatenate([t.reshape(128, -1, 4), np.zeros((128, 1, 4), BF)], axis=1)
    return np.ascontiguousarray(v[:, e]).reshape(128, -1)
def cut(t, i, w=512):
    return t[:, w * i:w * i + w]
def pick(q, e):
    c = np.concatenate([q[0].reshape(128, -1, 4), np.zeros((128, 1, 4), np.uint8)], axis=1); s = np.concatenate([q[1], np.ones((16, 1), np.uint8)], axis=1)
    return (np.ascontiguousarray(c[:, e].reshape(128, -1)), np.ascontiguousarray(s[:, e]))
def join(*qs):
    return (np.concatenate([q[0] for q in qs], axis=1), np.concatenate([q[1] for q in qs], axis=1))
def put(q, e, v):
    c, s = q[0].reshape(128, -1, 4).copy(), q[1].copy(); c[:, e] = v[0].reshape(128, -1, 4); s[:, e] = v[1]
    return (c.reshape(128, -1), s)
def pk(c, s):
    return (np.ascontiguousarray(c), mx_ref.live(s))
def emit(q):
    return q[0], q[1]
def decode(q):
    o = []
    for b in range(4):
        e = np.zeros((128, 128, 4), np.float32); e[np.arange(128), np.arange(128), b] = 1
        o.append(mx_ref.matmul(mx_ref.quantize(e.reshape(128, 512).astype(BF)), q))
    return np.stack(o, axis=2).reshape(128, -1)
def f(rng, *shape):
    return mx_ref.flush((rng.standard_normal(shape, dtype=np.float32) * np.exp2(rng.integers(-2, 3, shape[:-1] + (1,)))).astype(BF))
def wide(rng, *shape, cols=0):
    v = rng.standard_normal(shape, dtype=np.float32) * np.exp2(rng.integers(-12, 13, shape)).astype(np.float32)
    if cols: v *= np.repeat(np.exp2(rng.integers(-cols, cols + 1, shape[:-2] + (1, shape[-1] // 4))) * (rng.random(shape[:-2] + (1, shape[-1] // 4)) > 0.0625), 4, axis=-1).astype(np.float32)
    return mx_ref.flush(v.astype(BF))
T, C = 256, 64
def best(s):
    return np.argsort(-(s + np.float32(0)), kind="stable")[:C]
def quant(u, v):
    qu = [mx_ref.quantize(np.ascontiguousarray(u[r])) for r in range(N)]
    return qu, [[mx_ref.quantize(np.ascontiguousarray(cut(v[r], i))) for i in range(4)] for r in range(N)]
def layer(q, qu, qv):
    e = best(mx_ref.matmul(qu, q)[0])
    old = pick(q, e)
    a = np.stack([mx_ref.matmul(t, old) for t in qv], axis=2)
    new = np.maximum(a, np.float32(0)) * np.float32(0.05) + decode(old).reshape(128, C, 4)
    return e, new.reshape(128, -1).astype(BF)
def setup_inputs(rng):
    u = np.zeros((N, 128, 512), BF)
    u[:, :, :4] = f(rng, N, 128, 4)
    return {"x": f(rng, N, 128, 4 * T), "u": u, "v": f(rng, N, 128, 2048), "w": f(rng, N, 128, 512)}
def setup_inputs_spread(rng):
    d = setup_inputs(rng)
    d["x"] = wide(rng, N, 128, 4 * T, cols=3)
    return d
def setup_inputs_ties(rng):
    d = setup_inputs(rng)
    d["x"] = np.stack([cols(d["x"][r], rng.permutation(T) % 5 - 1) for r in range(N)])
    d["u"][1::2] = 0
    return d
def setup_inputs_again(rng):
    d = setup_inputs(rng)
    x, u = d["x"].astype(np.float32).reshape(N, 128, T, 4), np.zeros((N, 128, 512), np.float32)
    good = np.stack([rng.permutation(T) < C for r in range(N)])
    x[:, :32] = (1 + rng.random((N, 32, T, 4))) * np.where(good, 1.0, -1.0)[:, None, :, None]
    u[:, :32, :4] = 1 + rng.random((N, 32, 4))
    d["x"], d["u"] = x.reshape(N, 128, 4 * T).astype(BF), u.astype(BF)
    return d
def setup_inputs_other(rng):
    d = setup_inputs(rng)
    x, u = d["x"].astype(np.float32).reshape(N, 128, T, 4), np.zeros((N, 128, 512), np.float32)
    v = d["v"].astype(np.float32).reshape(N, 128, 4, 128, 4)
    large = np.stack([rng.permutation(T) < C for r in range(N)])
    x[:, :16] = (1 + rng.random((N, 16, T, 4))) * np.where(large, 16.0, 1.0)[:, None, :, None]
    x[:, 16:32] = (0.25 + 0.25 * rng.random((N, 16, T, 4))) * rng.choice([-1.0, 1.0], (N, 16, T, 4))
    u[:, :16, :4] = 1 + rng.random((N, 16, 4))
    u[:, 16:32, :4] = -1 - rng.random((N, 16, 4))
    v[:, :, :, 16:32] = 0
    v[:, :16, :, 16:32] = 256 * (1 + rng.random((N, 16, 4, 16, 4)))
    d["x"], d["u"], d["v"] = x.reshape(N, 128, 4 * T).astype(BF), u.astype(BF), v.reshape(N, 128, 2048).astype(BF)
    return d
def setup_inputs_neg(rng):
    d = setup_inputs(rng)
    d["x"] = np.abs(d["x"].astype(np.float32)).astype(BF)
    d["v"] = (-np.abs(d["v"].astype(np.float32))).astype(BF)
    return d
def check_inputs(d):
    b = []
    for k in ("x", "u", "v", "w"):
        a = np.abs(d[k].astype(np.float32))
        if not (np.isfinite(a).all() and ((a == 0) | (a >= 2.0 ** -30) & (a <= 2.0 ** 30)).all()): b.append("a value of " + k)
    if (d["u"][:, :, 4:].astype(np.float32) != 0).any(): b.append("u has numbers behind its column 0")
    if b: return b
    qu, qv = quant(d["u"], d["v"])
    for r in range(N):
        q = mx_ref.quantize(np.ascontiguousarray(d["x"][r]))
        for k in (1, 2):
            e, new = layer(q, qu[(r + k) % N], qv[(r + k) % N])
            a = np.abs(new.astype(np.float32)).reshape(16, 8, C, 4).max(axis=(1, 3))
            if not ((a == 0) | (a >= 2.0 ** -30) & (a <= 2.0 ** 30)).all(): return ["a number of a made column"]
            q = put(q, e, mx_ref.quantize(new))
    return b
def reference(x, u, v, w):
    oc, osc = np.zeros((N, 128, 4 * T), np.uint8), np.zeros((N, 16, T), np.uint8)
    li, y = np.zeros((N, 2, C), np.float32), np.zeros((N, 128, T), np.float32)
    qu, qv = quant(u, v)
    for d in range(N):
        r = (d - 2) % N
        q = mx_ref.quantize(np.ascontiguousarray(x[r]))
        for k in (1, 2):
            s = (r + k) % N
            e, new = layer(q, qu[s], qv[s])
            q = put(q, e, mx_ref.quantize(new))
            li[d, k - 1] = e
        oc[d], osc[d] = emit(q)
        y[d] = mx_ref.matmul(mx_ref.quantize(np.ascontiguousarray(w[d])), q)
    return {"oc": oc, "osc": osc, "li": li, "y": y}

from concourse.bass import DstId, RemoteDMATransfer
from concourse.mybir import dt, AluOpType, AxisListType, ActivationFunctionType

A = AluOpType
AF = ActivationFunctionType
F8, U8, BF, F32, I32, U16 = "float8_e4m3fn_x4", "uint8", "bfloat16", "float32", "int32", "uint16"
EPS = 2.0 ** -110
XC = 48
TC = 64
W2 = 576

SCRATCH = {}


def _pair(n, w):
    SCRATCH[n] = ("sbuf", [128, w], F8)
    SCRATCH[n + "s"] = ("sbuf", [128, w], U8)


for _n, _w in (("uq", 128), ("vq", 512), ("wq", 128), ("eq", 512), ("kq", 128), ("jq", 128), ("tq", 256), ("ul", 8),
               ("ub", 128), ("nb", 256), ("aw", W2), ("bw", W2), ("x1q", 128), ("x2q", 128), ("t1", 256), ("t2", 256),
               ("oh1q", 128), ("oh2q", 128)):
    _pair(_n, _w)
for _n, _w, _d in (("xt", 1024, BF), ("ut", 512, BF), ("vt", 2048, BF), ("wt", 512, BF), ("zt", 520, BF), ("idn", 128, BF),
                   ("kt", 512, BF), ("jt", 512, BF), ("x1b", 512, BF), ("x2b", 512, BF), ("oh1", 512, BF), ("oh2", 512, BF),
                   ("rl1", 1024, F32), ("rl2", 1024, F32), ("n1b", 1024, BF), ("n2b", 1024, BF), ("g1", 512, BF), ("g2", 512, BF),
                   ("sc1", 256, BF), ("sc2", 256, BF), ("tb", 384, F32), ("cx", 24, F32), ("x16", 16, F32), ("i16", 128, F32),
                   ("rm", 128, F32), ("ii", 128, I32), ("ij", 128, I32), ("pc", 1, I32), ("pl", 1, I32), ("zo", 16, U16),
                   ("oo", 16, U16), ("off1", 16, U16), ("off2", 16, U16), ("pl1", 1, F32), ("pl2", 1, F32), ("ll1", 1, F32),
                   ("ll2", 1, F32), ("yt", 256, F32)):
    SCRATCH[_n] = ("sbuf", [128, _w], _d)
for _n, _w in (("pr", 1024), ("pm", 2048), ("po", 512), ("pp", 512)):
    SCRATCH[_n] = ("psum", [128, _w], F32)

NEV = 130
SEMAPHORES = ["s%d" % _i for _i in range(NEV)] + ["lo", "ru", "rt0", "rx1", "rl1", "rt1", "rx2", "rl2", "gate", "gate2"]


def rank_program(g, core, T, topo):
    rank = T.rank_of(core)
    if rank is None:
        return
    n = len(T.cores)
    nxt, nx2, prv = T.cores[(rank + 1) % n], T.cores[(rank + 2) % n], T.cores[(rank - 1) % n]
    Q = {"g": g, "v": g.vector, "a": g.scalar, "s": g.sync, "t": g.tensor}
    V, S, P, Y = g.vector, g.scalar, g.tensor, g.sync
    made, known, nloc = [], {}, [0]

    def ev(ins, k=1, e=None):
        if e is None:
            e = ["s%d" % len(made), 0]
            made.append(e)
        ins.then_inc(T.sem[e[0]], k)
        e[1] += k
        return e

    def evs(*ins):
        e = None
        for i in ins:
            e = ev(i, 1, e)
        return e

    def wt(q, *es):
        for e in es:
            if e is not None and (q, e[0]) not in known:
                known[(q, e[0])] = 1
                Q[q].wait_ge(T.sem[e[0]], e[1])

    def zero(*bufs):
        return evs(*[V.memset(b[:], 0.0) for b in bufs])

    def bits(es):
        m = 0
        for e in es:
            m |= 1 << e
        return m

    def send(dst, out, in_, sem):
        rid, pid, _ = topo.addr(dst)
        g.remote_dma(out, in_, T.sem[sem], T.sem.lo, pid, rid, topo.mask(core, dst))
        k = len(topo.engines(core, dst))
        nloc[0] += k
        return k

    def send2(dst, pairs, sem):
        rid, pid, _ = topo.addr(dst)
        es = topo.engines(core, dst)
        h = len(es) // 2
        g.remote_dma_fused([RemoteDMATransfer(dst_ids=[DstId(rid=rid, pnc=pid)], dma_engine_mask=bits(es[i * h:i * h + h]),
                                              remote_sem=T.sem[sem], srcs=[s], dsts=[d], alu_op=0)
                            for i, (d, s) in enumerate(pairs)], local_sem=T.sem.lo)
        nloc[0] += 2 * h
        return (sem, 2 * h)

    def u8(v):
        return v.bitcast(dt.uint8)

    def u32(v):
        return v.bitcast(dt.uint32)

    def load_v(i, j):
        return ev(Y.dma_start(T.vt[:, 512 * i:512 * j], T.v[:, 512 * i:512 * j]), 16)

    e_u = ev(S.dma_start(T.ut[:, 0:4], T.u[:, 0:4]), 16)
    e_x = [ev(Y.dma_start(T.xt[:, 512 * i:512 * i + 512], T.x[:, 512 * i:512 * i + 512]), 16) for i in range(2)]
    e_v = [load_v(0, 1)]

    e_tb0 = evs(V.memset(T.tb[:, 128:384], 0.0))
    e_cx = evs(V.memset(T.cx[:], 64.0))
    e_id = evs(V.memset(T.idn[:], 1.0))
    e_tb1 = evs(V.memset(T.tb[:, 0:128], -EPS))
    e_u0 = evs(V.memset(T.ut[:, 8:512], 0.0))
    e_zo = evs(V.memset(T.zo[:], 0), V.memset(T.oo[:], 1))
    wt("g", e_tb0)
    e_tb2 = ev(g.affine_select(T.tb[:, 128:256], T.tb[:, 128:256], [[1, 128]], A.is_ge, -EPS, 0, -1))
    wt("g", e_cx)
    e_cx = ev(g.affine_select(T.cx[:], T.cx[:], [[-16, 24]], A.is_ge, -1.0, 128, 1))
    wt("g", e_cx)
    e_cx = ev(g.affine_select(T.cx[:], T.cx[:], [[16, 24]], A.is_ge, -1.0, 15 - 128, -1))
    e_16 = ev(g.iota(T.x16[:], [[16, 16]], 0, 0, allow_small_or_imprecise_dtypes=True))
    wt("g", e_id)
    e_id = ev(g.affine_select(T.idn[:], T.idn[:], [[1, 128]], A.is_equal, 0.0, 0, -1))
    e_ii = ev(g.iota(T.ii[:], [[1, 128]], 128, -1))
    e_xz = zero(T.x1b, T.x2b)
    e_zz = zero(T.zt)

    wt("v", e_u, e_u0)
    e_nu = ev(V.tensor_scalar(T.ut[:, 4:8], T.ut[:, 0:4], -1.0, None, A.mult))
    wt("v", e_nu)
    e_uq = ev(V.quantize_mx(T.uq[:], T.uqs[:], T.ut[:]))
    wt("g", e_uq)
    r_u = send2(prv, [(u8(T.ul[:, 0:2]), u8(T.uq[:, 0:2])), (T.uls[:, 0:8], T.uqs[:, 0:8])], "ru")
    e_kz = zero(T.kt, T.jt)

    e_t = []
    for i in range(2):
        wt("v", e_x[i])
        e_t.append(ev(V.quantize_mx(T.tq[:, 128 * i:128 * i + 128], T.tqs[:, 128 * i:128 * i + 128], T.xt[:, 512 * i:512 * i + 512])))
    wt("g", *e_t)
    k = send(nxt, T.aws[:, TC:TC + 256], T.tqs[:], "rt0")
    g.sem_inc(T.sem.gate, 1)
    k += send(nxt, u8(T.aw[:, TC:TC + 256]), u8(T.tq[:]), "rt0")
    r_t0 = ("rt0", k)
    wt("s", ("gate", 1))
    e_v += [load_v(1, 2), load_v(2, 4)]
    e_i6 = ev(g.iota(T.i16[:], [[0, 8], [1, 16]], 0, 0, allow_small_or_imprecise_dtypes=True))
    e_pc = ev(g.iota(T.pc[:], [[1, 1]], 0, 1))
    e_rm = ev(g.iota(T.rm[:], [[1, 128]], 0, 0, allow_small_or_imprecise_dtypes=True))

    wt("v", e_id, e_zz)
    e_zc = ev(V.tensor_copy(T.zt[:, 4:516:4], T.idn[:]))
    wt("v", e_xz)
    e_xc = evs(*[V.memset(b[0:2, 4 * XC + 2:4 * XC + 64:4], 1.0) for b in (T.x1b, T.x2b)])
    wt("v", e_ii)
    e_ij = ev(V.tensor_scalar(T.ij[:], T.ii[:], 15, None, A.bitwise_and))
    wt("v", e_zc)
    e_e = [ev(V.quantize_mx(T.eq[:, 128 * b:128 * b + 128], T.eqs[:, 128 * b:128 * b + 128], T.zt[:, 4 - b:516 - b])) for b in range(4)]
    wt("v", e_16, e_xc)
    e_xc = evs(*[V.tensor_copy(b[0:1, 4 * XC + 2:4 * XC + 64:4], T.x16[0:1, :]) for b in (T.x1b, T.x2b)])
    wt("v", e_ij, e_kz)
    e_k = evs(*[V.tensor_scalar(T.kt[:, t:512:4], T.ij[:], 0.0, 256.0, A.is_equal, A.mult) for t in range(2)])
    wt("v", e_i6)
    e_k6 = ev(V.tensor_copy(T.kt[0:2, 2:512:4], T.i16[0:2, :]))
    wt("v", e_k6)
    ev(V.memset(T.kt[0:1, 2:512:4], 1.0), 1, e_k)
    wt("v", e_k)
    e_kq = ev(V.quantize_mx(T.kq[:], T.kqs[:], T.kt[:]))

    def quant_v(k, i, j):
        wt("v", e_v[k])
        return ev(V.quantize_mx(T.vq[:, 128 * i:128 * j], T.vqs[:, 128 * i:128 * j], T.vt[:, 512 * i:512 * j]))

    e_vq = [quant_v(0, 0, 1)]

    wt("v", r_u, e_zo)
    wt("a", r_u, e_zo)
    e_ub = evs(V.tensor_copy(u32(T.ub[:]), u32(T.ul[:, 0:2]).indirect(T.zo[:, 0:8])),
               S.activation(T.ubs[:], T.uls[:, 0:2].indirect(T.zo[:, 0:8]), AF.Copy))
    e_nb = evs(V.tensor_copy(u32(T.nb[:]), u32(T.ul[:, 0:2]).indirect(T.oo[:, 0:16])),
               S.activation(T.nbs[:], T.uls[:, 0:2].indirect(T.oo[:, 0:16]), AF.Copy))

    def ranking(q, qs, ready, free, gb, sc, xb, xq, xqs):
        wt("t", *ready)
        e_r = []
        for h in range(2):
            wt("t", free[h], e_ub)
            o = T.pr[:, 512 * h:512 * h + 256]
            P.matmul_mx(o, T.ub[:], T.ubs[:], q[:], qs[:], True, False)
            wt("t", e_nb)
            e_r.append(ev(P.matmul_mx(o, q[:, 128 * h:128 * h + 128], qs[:, 128 * h:128 * h + 128], T.nb[:], T.nbs[:], False, True)))
        wt("v", e_tb1, e_tb2)
        e_c = []
        for h in range(2):
            wt("v", e_r[h])
            e_c.append(ev(V.tensor_tensor(gb[:, 256 * h:256 * h + 256], T.pr[:, 512 * h:512 * h + 256],
                                          T.tb[:, 128 - 128 * h:384 - 128 * h], A.is_gt)))
        e_s = []
        for h in range(2):
            wt("v", e_c[h])
            e_s.append(ev(V.tensor_tensor_scan(sc[:, 128 * h:128 * h + 128], gb[:, 256 * h:256 * h + 128],
                                               gb[:, 256 * h + 128:256 * h + 256], 0.0, A.add, A.add)))
        wt("v", e_cx, e_xc)
        e_f = None
        for h in range(2):
            wt("v", e_s[h])
            e_f = ev(V.tensor_scalar(xb[:, 4 * XC + h:4 * XC + 64:4], T.cx[:, 8 - 8 * h:24 - 8 * h],
                                     sc[:, 128 * h + 127:128 * h + 128], None, A.is_gt), 1, e_f)
        wt("v", e_f)
        return ev(V.quantize_mx(xq[:], xqs[:], xb[:])), e_c, e_s

    def send_flags(w, ws, xq, xqs, sem):
        return send2(nxt, [(u8(w[:, XC:XC + 16]), u8(xq[:, XC:XC + 16])), (ws[:, 0:64], xqs[:, 0:64])], sem)

    e_x1, e_c1, e_s1 = ranking(T.tq, T.tqs, e_t, (None, None), T.g1, T.sc1, T.x1b, T.x1q, T.x1qs)
    wt("g", e_x1)
    r_x1 = send_flags(T.aw, T.aws, T.x1q, T.x1qs, "rx1")
    e_vq += [quant_v(1, 1, 2), quant_v(2, 2, 4)]

    def make(w, ws, arrived, rl, nb, free, between=None):
        e_a, e_r = [], []
        wt("t", arrived)
        for i in range(4):
            b = 1024 * (i % 2)
            wt("t", e_vq[min(i, 2)], *(free[i] if i < 2 else (e_r[i - 2], e_a[i - 2])))
            e_1 = ev(P.matmul_mx(T.pm[:, b:b + 256], T.vq[:, 128 * i:128 * i + 128], T.vqs[:, 128 * i:128 * i + 128],
                                 w[:, TC:TC + 256], ws[:, TC:TC + 256], True, True))
            wt("t", e_e[i])
            e_2 = ev(P.matmul_mx(T.pm[:, b + 512:b + 768], T.eq[:, 128 * i:128 * i + 128], T.eqs[:, 128 * i:128 * i + 128],
                                 w[:, TC:TC + 256], ws[:, TC:TC + 256], True, True))
            wt("a", e_1)
            e_r.append(ev(S.activation(rl[:, 256 * i:256 * i + 256], T.pm[:, b:b + 256], AF.Relu, scale=0.05)))
            wt("v", e_2, e_r[i])
            e_a.append(ev(V.tensor_tensor(nb[:, i:1024:4], T.pm[:, b + 512:b + 768], rl[:, 256 * i:256 * i + 256], A.add)))
            if i == 1 and between is not None:
                between()
        wt("v", *e_a)
        e_n = ev(V.quantize_mx(w[:, TC + 256:TC + 512], ws[:, TC + 256:TC + 512], nb[:]))
        return e_n, [(e_r[2], e_a[2]), (e_r[3], e_a[3])]

    def choose(w, ws, e_n, r_x, off, t, ts, free):
        wt("t", r_x, e_kq, free)
        e_o = ev(P.matmul_mx(T.po[:, 0:128], T.kq[:], T.kqs[:], w[:, XC:XC + 128], ws[:, XC:XC + 128], True, True))
        wt("v", e_o)
        e_of = ev(V.tensor_copy(off[:], T.po[:, 0:16]))
        wt("v", e_of, e_n)
        wt("a", e_of, e_n)
        e_c = ev(V.tensor_copy(u32(t[:]), u32(w[:, TC:TC + 512]).indirect(off[:, 0:16])))
        e_p = ev(S.activation(ts[:], ws[:, TC:TC + 512].indirect(off[:, 0:16]), AF.Copy))
        return [e_c, e_p], e_of

    e_n1, fr = make(T.aw, T.aws, r_t0, T.rl1, T.n1b, [(), ()])
    e_t1, e_o1 = choose(T.aw, T.aws, e_n1, r_x1, T.off1, T.t1, T.t1s, None)
    wt("g", e_t1[0])
    k = send(nxt, u8(T.bw[:, TC:TC + 256]), u8(T.t1[:]), "rt1")
    wt("g", e_t1[1])
    k += send(nxt, T.bws[:, TC:TC + 256], T.t1s[:], "rt1")
    r_t1 = ("rt1", k)

    g.sem_inc(T.sem.gate2, 1)
    wt("s", ("gate2", 1))
    e_w = ev(Y.dma_start(T.wt[:], T.w[:]), 16)

    e_x2, e_c2, e_s2 = ranking(T.t1, T.t1s, e_t1, e_c1, T.g2, T.sc2, T.x2b, T.x2q, T.x2qs)
    wt("g", e_x2)
    r_x2 = send_flags(T.bw, T.bws, T.x2q, T.x2qs, "rx2")

    wt("v", e_pc, e_kz)
    e_pl = ev(V.tensor_scalar(T.pl[:], T.pc[:], 15, None, A.bitwise_and))
    e_hz = zero(T.oh1, T.oh2)
    wt("v", e_pl)
    e_j = evs(V.tensor_copy(T.jt[:, 0:1], T.pl[:]), V.tensor_copy(T.jt[:, 1:2], T.pl[:]),
              V.tensor_tensor(T.jt[:, 4:5], T.pc[:], T.pl[:], A.subtract))
    wt("v", e_rm, e_hz, *e_s1)
    e_h1 = evs(*[V.tensor_scalar(T.oh1[:, h:512:4], T.rm[:], T.sc1[:, 128 * h + 127:128 * h + 128], None, A.is_equal) for h in range(2)])
    wt("v", e_j)
    e_j = ev(V.tensor_scalar(T.jt[:, 5:6], T.jt[:, 4:5], 128.0, None, A.add))
    wt("v", *e_s2)
    e_h2 = evs(*[V.tensor_scalar(T.oh2[:, h:512:4], T.rm[:], T.sc2[:, 128 * h + 127:128 * h + 128], None, A.is_equal) for h in range(2)])
    wt("v", e_j)
    e_jq = ev(V.quantize_mx(T.jq[:], T.jqs[:], T.jt[:]))
    wt("v", e_h1)
    e_h1 = ev(V.quantize_mx(T.oh1q[:], T.oh1qs[:], T.oh1[:]))
    wt("v", e_h2)
    e_h2 = ev(V.quantize_mx(T.oh2q[:], T.oh2qs[:], T.oh2[:]))
    wt("t", e_jq, e_h1)
    e_p1 = ev(P.matmul_mx(T.pp[:, 0:128], T.oh1q[:], T.oh1qs[:], T.jq[:], T.jqs[:], True, True))
    wt("v", e_p1)
    e_l1 = ev(V.tensor_reduce(T.pl1[:], T.pp[:, 0:2], AxisListType.X, A.add))
    wt("t", e_h2, e_l1)
    e_p2 = ev(P.matmul_mx(T.pp[:, 0:128], T.oh2q[:], T.oh2qs[:], T.jq[:], T.jqs[:], True, True))
    wt("v", e_p2)
    e_l2 = ev(V.tensor_reduce(T.pl2[:], T.pp[:, 0:2], AxisListType.X, A.add))
    wt("g", e_l1)
    r_l1 = ("rl1", send(nx2, T.ll1[:], T.pl1[:], "rl1"))
    wt("g", e_l2)
    r_l2 = ("rl2", send(nxt, T.ll2[:], T.pl2[:], "rl2"))

    e_wq = []

    def quant_w():
        wt("v", e_w)
        e_wq.append(ev(V.quantize_mx(T.wq[:], T.wqs[:], T.wt[:])))

    e_n2, fr = make(T.bw, T.bws, r_t1, T.rl2, T.n2b, fr, quant_w)
    e_t2, e_o2 = choose(T.bw, T.bws, e_n2, r_x2, T.off2, T.t2, T.t2s, e_o1)

    wt("s", e_t2[0])
    e_out = ev(Y.dma_start(T.oc[:], u8(T.t2[:])), 16)
    e_y = []
    wt("t", *e_wq, *e_t2)
    for h in range(2):
        wt("t", e_c2[h])
        e_y.append(ev(P.matmul_mx(T.pr[:, 512 * h:512 * h + 128], T.wq[:], T.wqs[:], T.t2[:, 128 * h:128 * h + 128],
                                  T.t2s[:, 128 * h:128 * h + 128], True, True)))
    wt("v", e_y[0])
    e_z0 = ev(V.tensor_copy(T.yt[:, 0:128], T.pr[:, 0:128]))
    wt("a", e_y[1])
    e_z1 = ev(S.activation(T.yt[:, 128:256], T.pr[:, 512:640], AF.Copy))
    wt("s", e_t2[1])
    for q in range(4):
        ev(Y.dma_start(T.osc[4 * q:4 * q + 4, :], T.t2s[32 * q:32 * q + 4, :]), 16, e_out)
    wt("s", e_z0)
    ev(Y.dma_start(T.y[:, 0:128], T.yt[:, 0:128]), 16, e_out)
    wt("a", e_z1)
    ev(S.dma_start(T.y[:, 128:256], T.yt[:, 128:256]), 16, e_out)
    wt("a", r_l1)
    ev(S.dma_start(T.li[0:1, :], T.ll1[0:64, 0:1]), 16, e_out)
    wt("a", r_l2)
    ev(S.dma_start(T.li[1:2, :], T.ll2[0:64, 0:1]), 16, e_out)

    done = {e for (_, e) in known}
    wt("s", *[e for e in made if e[0] not in done])
    g.wait_ge(T.sem.lo, nloc[0])
